import numpy as np
import ml_dtypes


def mxq(x, axis, fmt="e4m3"):
    dtype, down = {"e4m3": (ml_dtypes.float8_e4m3fn, 7), "e5m2": (ml_dtypes.float8_e5m2, 14)}[fmt]
    v = np.moveaxis(np.asarray(x, np.float32).astype(ml_dtypes.bfloat16).astype(np.float64), axis, -1)
    blocks = v.reshape(v.shape[:-1] + (-1, 32))
    amax = np.abs(blocks).max(-1, keepdims=True)
    byte = np.maximum(np.where(amax > 0, np.frexp(amax)[1] - 1 + 127, 0) - down, 1)
    scale = np.exp2(byte - 127.0)
    codes = (blocks / scale).astype(np.float32).astype(dtype).astype(np.float64)
    return np.moveaxis((codes * scale).reshape(v.shape), -1, axis)


WIDE = False


def mx_kscale(k):
    if not WIDE:
        return np.ones(k)
    levels = np.array([10, -10, 5, -5, 0])
    if k % 512:
        return np.exp2(np.random.permutation(np.resize(levels, k // 32))).repeat(32)
    a = np.empty((k // 512, 16))
    for p in range(k // 512):
        a[p, :8] = np.random.permutation(np.resize(levels, 8))
        for g in range(8):
            far = levels[np.abs(levels - a[p, g]) >= 10]
            a[p, g + 8] = far[np.random.randint(len(far))]
    return np.exp2(a.ravel()).repeat(32)


def f64(x):
    return np.asarray(x).astype(np.float64)


def striped(idx):
    return np.tile(np.asarray(idx).reshape(-1, 16).T, (8, 1)).astype(np.uint16)


def unstriped(offs):
    return offs[:16].T.reshape(-1).astype(np.int64)


def striped8(idx):
    return np.asarray(idx).reshape(8, -1, 16).transpose(0, 2, 1).reshape(128, -1).astype(np.uint16)


def unstriped8(offs):
    return offs.reshape(8, 16, -1).transpose(0, 2, 1).reshape(8, -1).astype(np.int64)


def pick8(x, idx, run):
    r = np.arange(len(x))
    return x[r[:, None], idx[r % (8 * run) // run]]


E2M1 = np.array([0.0, 0.5, 1.0, 1.5, 2.0, 3.0, 4.0, 6.0, -0.0, -0.5, -1.0, -1.5, -2.0, -3.0, -4.0, -6.0])


def pack_weight(w, fmt):
    k, n = w.shape
    w = f64(np.asarray(w, np.float32).astype(ml_dtypes.bfloat16)).reshape(k // 32, 32, n)
    amax = np.abs(w).max(1)
    if fmt == "e4m3":
        byte = np.frexp(amax)[1] - 1 + 127 - 7
    else:
        mant, ex = np.frexp(amax / 6.0)
        byte = np.where(mant > 0.5, ex, ex - 1) + 127
    byte = np.clip(np.where(amax > 0, byte, 1), 1, 254)
    scaled = (w * np.exp2(127.0 - byte)[:, None, :]).reshape(k, n).astype(np.float32)
    by_word = np.ascontiguousarray(scaled.reshape(k // 512, 128, 4, n).transpose(0, 1, 3, 2))
    if fmt == "e4m3":
        words = by_word.astype(ml_dtypes.float8_e4m3fn).view(np.uint8)
    else:
        c = by_word.astype(ml_dtypes.float4_e2m1fn).view(np.uint8) & 0xF
        words = (c[..., 0::2] | (c[..., 1::2] << 4)).reshape(k // 512, 128, 2 * n)
    return np.ascontiguousarray(words), np.ascontiguousarray(byte.astype(np.uint8).reshape(k // 512, 16, n))


def unpack_weight(words, scales, fmt):
    g, _, n = scales.shape
    words = np.ascontiguousarray(words).reshape(g, 128, n, -1)
    if fmt == "e4m3":
        vals = words.view(ml_dtypes.float8_e4m3fn).astype(np.float64)
    else:
        nib = np.empty((g, 128, n, 4), np.uint8)
        nib[..., 0::2] = words & 0xF
        nib[..., 1::2] = words >> 4
        vals = E2M1[nib]
    vals = vals * np.repeat(np.exp2(scales.astype(np.float64) - 127.0), 8, axis=1)[..., None]
    return vals.transpose(0, 1, 3, 2).reshape(g * 512, n)


K, J, R, T, Z, M, S, C, N, V = 512, 512, 512, 1024, 512, 1024, 256, 512, 256, 1024


def setup_inputs():
    n = np.random.standard_normal
    idx = np.random.permutation(T)[:J]
    idx2 = np.random.permutation(M)[:J]
    idx3 = np.stack([np.random.permutation(J)[:S] for _ in range(8)])
    idx4 = np.stack([np.random.permutation(J)[:S] for _ in range(8)])
    idx5 = np.stack([np.random.permutation(C)[:S] for _ in range(8)])
    idx6 = np.random.permutation(V)[:N]
    fk = mx_kscale(K)
    fr = mx_kscale(R)
    fz = mx_kscale(Z)
    xtp = pack_weight(n((K, T)) * fk[:, None], "e4m3")
    wp = pack_weight(n((K, R)) * 1 / np.sqrt(K) / fk[:, None] * fr, "e4m3")
    xop = pack_weight(n((Z, M)) / fz[:, None], "e4m3")
    w2p = pack_weight(n((Z, R)) * 1 / np.sqrt(Z) * fz[:, None] * fr, "e2m1")
    vsp = pack_weight(n((R, V)) * 1 / np.sqrt(R) / fr[:, None], "e2m1")
    return {
        "xt_words": xtp[0],
        "xt_scales": xtp[1],
        "w_words": wp[0],
        "w_scales": wp[1],
        "xo_words": xop[0],
        "xo_scales": xop[1],
        "w2_words": w2p[0],
        "w2_scales": w2p[1],
        "sa": (np.random.uniform(0.5, 1.6, (R, 1))).astype(np.float32),
        "sb": (np.random.uniform(0.5, 1.6, (R, 1))).astype(np.float32),
        "vs_words": vsp[0],
        "vs_scales": vsp[1],
        "offs": striped(idx),
        "offs2": striped(idx2),
        "offs3": striped8(idx3),
        "offs4": striped8(idx4),
        "offs5": striped8(idx5),
        "offs6": striped(idx6),
    }


def reference(xt_words, xt_scales, w_words, w_scales, xo_words, xo_scales, w2_words, w2_scales, sa, sb, vs_words, vs_scales, offs, offs2, offs3, offs4, offs5, offs6):
    idx = unstriped(offs)
    idx2 = unstriped(offs2)
    idx3 = unstriped8(offs3)
    idx4 = unstriped8(offs4)
    idx5 = unstriped8(offs5)
    idx6 = unstriped(offs6)
    xtu = unpack_weight(xt_words, xt_scales, "e4m3")
    wu = unpack_weight(w_words, w_scales, "e4m3")
    xou = unpack_weight(xo_words, xo_scales, "e4m3")
    w2u = unpack_weight(w2_words, w2_scales, "e2m1")
    vsu = unpack_weight(vs_words, vs_scales, "e2m1")
    xtidxg = xtu[:, idx]
    a = wu.T @ xtidxg
    xoidx2g = xou[:, idx2]
    b = w2u.T @ xoidx2g
    h1 = np.maximum(pick8(a, idx3, 64) * f64(sa), pick8(b, idx4, 64) * f64(sb))
    hid = np.zeros((R, C))
    hid[np.arange(R)[:, None], idx5[np.arange(R) % 512 // 64]] = h1
    vsidx6g = vsu[:, idx6]
    hidq = mxq(hid, 0, "e4m3")
    y = vsidx6g.T @ hidq
    return y

@@ -1,0 +1,217 @@
+from contextlib import ExitStack
+
+import concourse.mybir as mybir
+
+F32 = mybir.dt.float32
+BF16 = mybir.dt.bfloat16
+I32 = mybir.dt.int32
+U32 = mybir.dt.uint32
+U16 = mybir.dt.uint16
+U8 = mybir.dt.uint8
+FP8X4 = mybir.dt.float8_e4m3fn_x4
+FP4X4 = mybir.dt.float4_e2m1fn_x4
+COPY = mybir.ActivationFunctionType.Copy
+MAX = mybir.AluOpType.max
+
+P = 128
+PACK = 4
+J, R, T, M, S, C, N, V = 512, 512, 1024, 1024, 256, 512, 256, 1024
+HALF = 256
+
+FLOPS = 2 * 512 * R * J * 2 + 2 * R * N * C
+
+
+def tile_picked_tokens_plain_two_pairpost_store_plain_kernel(
+    tc, xt_words, xt_scales, w_words, w_scales, xo_words, xo_scales, w2_words, w2_scales, sa, sb,
+    vs_words, vs_scales, offs, offs2, offs3, offs4, offs5, offs6, out,
+):
+    nc = tc.nc
+    with ExitStack() as ctx:
+        keep = ctx.enter_context(tc.tile_pool(name="keep", bufs=1))
+        psum = ctx.enter_context(tc.psum_pool(name="psum", bufs=8))
+
+        def held(name, width, dtype):
+            return keep.tile([P, width], dtype, name=name, align_bytes=64)
+
+        def load_list(name, src):
+            tile = keep.tile([P, src.shape[1]], U16, name=name)
+            nc.sync.dma_start(tile[:], src)
+            return tile
+
+        def load_words(name, src, width, dtype):
+            tile = held(name, width, dtype)
+            nc.sync.dma_start(tile[:].bitcast(I32), src.bitcast(I32))
+            return tile
+
+        def load_scale_rows(tile, src):
+            for q in range(4):
+                nc.sync.dma_start(tile[32 * q : 32 * q + 4, :].bitcast(I32), src[0, 4 * q : 4 * q + 4, :].bitcast(I32))
+
+        def load_staged_rows(tile, first, src):
+            nc.sync.dma_start(
+                tile[first : first + 4, :].rearrange("r (q c) -> r q c", q=4),
+                src[0].bitcast(I32).rearrange("(q r) c -> r q c", q=4),
+            )
+
+        xt_s = held("xt_s", T, U8)
+        xo_s = held("xo_s", M, U8)
+        vs_s = held("vs_s", V, U8)
+        staged = held("staged", R, I32)
+        hid = [held("hid%d" % t, C, F32) for t in range(PACK)]
+        nc.gpsimd.memset(staged[0:32, :], 0)
+        nc.gpsimd.memset(xt_s[:].bitcast(I32), 0)
+        nc.vector.memset(xo_s[:].bitcast(I32), 0)
+        nc.vector.memset(vs_s[:].bitcast(I32), 0)
+        for t in range(PACK):
+            (nc.vector if t < 2 else nc.gpsimd).memset(hid[t][:], 0.0)
+
+        sa_t = keep.tile([P, PACK], F32, name="sa_t")
+        sb_t = keep.tile([P, PACK], F32, name="sb_t")
+
+        xo_staged = keep.tile([4, M], I32, name="xo_staged")
+        load_staged_rows(xo_staged, 0, xo_scales)
+        l2 = load_list("l2", offs2)
+        l4 = load_list("l4", offs4)
+        load_staged_rows(staged, 0, w2_scales)
+        load_staged_rows(staged, 4, w_scales)
+        xo_w = load_words("xo_w", xo_words[0].rearrange("p n t -> p (n t)"), M, U32)
+        w2_w = load_words("w2_w", w2_words[0], R, U16)
+        w_w = load_words("w_w", w_words[0].rearrange("p n t -> p (n t)"), R, U32)
+        xt_w = load_words("xt_w", xt_words[0].rearrange("p n t -> p (n t)"), T, U32)
+        l1 = load_list("l1", offs)
+        load_scale_rows(xt_s, xt_scales)
+        nc.sync.dma_start(sb_t[:], sb.rearrange("(p t) o -> p (t o)", t=PACK))
+        l3 = load_list("l3", offs3)
+        nc.sync.dma_start(sa_t[:], sa.rearrange("(p t) o -> p (t o)", t=PACK))
+        l5 = load_list("l5", offs5)
+        l6 = load_list("l6", offs6)
+        vs_w = load_words("vs_w", vs_words[0], V, U16)
+        load_scale_rows(vs_s, vs_scales)
+
+        xt_gw = held("xt_gw", J, U32)
+        xt_gs = held("xt_gs", J, U8)
+        xo_gw = held("xo_gw", J, U32)
+        xo_gs = held("xo_gs", J, U8)
+        w_dw = keep.tile([P, R], U32, name="w_dw", tag="words", align_bytes=64)
+        dealt_s = keep.tile([P, R], U8, name="dealt_s", tag="planes", align_bytes=64)
+        w2_dw = held("w2_dw", R, U16)
+        rows_a = [held("a%d" % t, J, F32) for t in range(PACK)]
+        rows_b = [held("b%d" % t, J, F32) for t in range(PACK)]
+        pick_a = [held("pa%d" % t, S, F32) for t in range(PACK)]
+        pick_b = [held("pb%d" % t, S, F32) for t in range(PACK)]
+        larger = [held("h%d" % t, S, F32) for t in range(PACK)]
+        hid16 = [held("hid16_%d" % h, PACK * HALF, BF16) for h in range(2)]
+        hq_w = [held("hq_w%d" % h, HALF, U32) for h in range(2)]
+        hq_s = [held("hq_s%d" % h, HALF, U8) for h in range(2)]
+        halves = [slice(h * HALF, (h + 1) * HALF) for h in range(2)]
+        whole = slice(0, J)
+
+        def deal_words(dst, src):
+            nc.scalar.copy(dst[:].rearrange("p (t m) -> p m t", t=PACK), src[:].rearrange("p (m t) -> p m t", t=PACK))
+
+        def deal_bytes(dst, src):
+            dealt = dst[:].rearrange("p (t m) -> p t m", t=PACK)
+            plain = src.rearrange("p (m t) -> p t m", t=PACK)
+            nc.gpsimd.tensor_copy(dealt[:, 0, :], plain[:, 0, :])
+            nc.gpsimd.tensor_copy(dealt[:, 1:PACK, :], plain[:, 1:PACK, :])
+
+        def gather_words(dst, src, lst):
+            for h in range(2):
+                nc.vector.tensor_copy(dst[:, halves[h]], src[:].indirect(lst[:, 16 * h : 16 * h + 16]))
+
+        def product(words, first, fmt, picked_words, picked_scales, t, cols):
+            acc = psum.tile([P, J], F32, name="acc")
+            nc.tensor.matmul_mx(
+                out=acc[:, cols],
+                lhsT=words[:, t * P : (t + 1) * P].bitcast(fmt),
+                lhsT_scale=dealt_s[first:P, t * P : (t + 1) * P],
+                rhs=picked_words[:, cols].bitcast(FP8X4),
+                rhs_scale=picked_scales[:, cols],
+                start=True,
+                stop=True,
+            )
+            return acc[:, cols]
+
+        def product_a(t, cols):
+            return product(w_dw, 4, FP8X4, xt_gw, xt_gs, t, cols)
+
+        def product_b(t, cols):
+            return product(w2_dw, 0, FP4X4, xo_gw, xo_gs, t, cols)
+
+        def fetch(dst, rows, lst, scale, t):
+            nc.scalar.activation(out=dst[t][:], in_=rows[t][:].indirect(lst[:]), func=COPY, scale=scale[:, t : t + 1])
+
+        def place(t):
+            nc.vector.tensor_tensor(larger[t][:], pick_a[t][:], pick_b[t][:], MAX)
+            nc.scalar.activation(out=hid[t][:].indirect(l5[:]), in_=larger[t][:], func=COPY)
+
+        def round_into_slot(t):
+            for h in range(2):
+                nc.vector.tensor_copy(hid16[h][:, t : PACK * HALF : PACK], hid[t][:, halves[h]])
+
+        for q in range(4):
+            nc.vector.tensor_copy(xo_s[32 * q : 32 * q + 4, :].bitcast(I32), xo_staged[:, q * (M // 4) : (q + 1) * (M // 4)])
+        width = R // 4
+        for q in range(1, 4):
+            nc.vector.tensor_copy(staged[32 * q : 32 * q + 32, 0:width], staged[0:32, q * width : (q + 1) * width])
+        nc.vector.tensor_copy(xo_gs[:], xo_s[:].indirect(l2[:]))
+        deal_bytes(dealt_s, staged[:, 0:width].bitcast(U8))
+        deal_words(w2_dw, w2_w)
+        gather_words(xo_gw, xo_w, l2)
+        deal_words(w_dw, w_w)
+
+        for cols in halves:
+            nc.scalar.activation(out=rows_b[0][:, cols], in_=product_b(0, cols), func=COPY)
+        for t in (1, 2):
+            nc.scalar.activation(out=rows_b[t][:], in_=product_b(t, whole), func=COPY)
+        acc_b3 = product_b(3, whole)
+
+        nc.vector.tensor_copy(xt_gs[:], xt_s[:].indirect(l1[:]))
+        gather_words(xt_gw, xt_w, l1)
+        for t in range(3):
+            fetch(pick_b, rows_b, l4, sb_t, t)
+
+        for cols in halves:
+            nc.vector.tensor_copy(rows_a[0][:, cols], product_a(0, cols))
+        fetch(pick_a, rows_a, l3, sa_t, 0)
+        nc.vector.tensor_copy(rows_a[1][:], product_a(1, whole))
+        fetch(pick_a, rows_a, l3, sa_t, 1)
+        place(0)
+        nc.vector.tensor_copy(rows_a[2][:], product_a(2, whole))
+        nc.vector.tensor_copy(rows_b[3][:], acc_b3)
+        fetch(pick_a, rows_a, l3, sa_t, 2)
+        place(1)
+        nc.vector.tensor_copy(rows_a[3][:], product_a(3, whole))
+        fetch(pick_b, rows_b, l4, sb_t, 3)
+        fetch(pick_a, rows_a, l3, sa_t, 3)
+        place(2)
+        round_into_slot(0)
+        place(3)
+        vs_gw = keep.tile([P, N], U16, name="vs_gw", tag="words", align_bytes=64)
+        vs_gs = keep.tile([P, N], U8, name="vs_gs", tag="planes", align_bytes=64)
+        nc.vector.tensor_copy(vs_gs[:], vs_s[:].indirect(l6[:]))
+        nc.vector.tensor_copy(vs_gw[:], vs_w[:].indirect(l6[:]))
+        round_into_slot(1)
+        round_into_slot(2)
+        round_into_slot(3)
+
+        for h in range(2):
+            nc.vector.quantize_mx(out=hq_w[h][:].bitcast(FP8X4), scales=hq_s[h][:], in_=hid16[h][:])
+        for h in range(2):
+            for j in range(2):
+                acc = psum.tile([P, J], F32, name="acc")
+                nc.tensor.matmul_mx(
+                    out=acc[:, 0:HALF],
+                    lhsT=vs_gw[:, j * P : (j + 1) * P].bitcast(FP4X4),
+                    lhsT_scale=vs_gs[:, j * P : (j + 1) * P],
+                    rhs=hq_w[h][:].bitcast(FP8X4),
+                    rhs_scale=hq_s[h][:],
+                    start=True,
+                    stop=True,
+                )
+                res = held("res%d%d" % (h, j), HALF, F32)
+                if h == 1 and j == 0:
+                    nc.vector.tensor_copy(res[:], acc[:, 0:HALF])
+                else:
+                    nc.scalar.activation(out=res[:], in_=acc[:, 0:HALF], func=COPY)
+                nc.sync.dma_start(out[j * P : (j + 1) * P, h * HALF : (h + 1) * HALF], res[:])

@@ -28,7 +28,7 @@ def tile_picked_tokens_plain_two_pairpost_store_plain_kernel(
     nc = tc.nc
     with ExitStack() as ctx:
         keep = ctx.enter_context(tc.tile_pool(name="keep", bufs=1))
-        psum = ctx.enter_context(tc.psum_pool(name="psum", bufs=8))
+        psum = ctx.enter_context(tc.psum_pool(name="psum", bufs=1))
 
         def held(name, width, dtype):
             return keep.tile([P, width], dtype, name=name, align_bytes=64)
@@ -43,14 +43,13 @@ def tile_picked_tokens_plain_two_pairpost_store_plain_kernel(
             nc.sync.dma_start(tile[:].bitcast(I32), src.bitcast(I32))
             return tile
 
-        def load_scale_rows(tile, src):
-            for q in range(4):
+        def load_scale_rows(tile, src, quarters):
+            for q in quarters:
                 nc.sync.dma_start(tile[32 * q : 32 * q + 4, :].bitcast(I32), src[0, 4 * q : 4 * q + 4, :].bitcast(I32))
 
-        def load_staged_rows(tile, first, src):
+        def load_staged_rows(rows, src):
             nc.sync.dma_start(
-                tile[first : first + 4, :].rearrange("r (q c) -> r q c", q=4),
-                src[0].bitcast(I32).rearrange("(q r) c -> r q c", q=4),
+                rows.rearrange("r (q c) -> r q c", q=src.shape[0] // 4), src.bitcast(I32).rearrange("(q r) c -> r q c", r=4)
             )
 
         xt_s = held("xt_s", T, U8)
@@ -59,9 +58,9 @@ def tile_picked_tokens_plain_two_pairpost_store_plain_kernel(
         staged = held("staged", R, I32)
         hid = [held("hid%d" % t, C, F32) for t in range(PACK)]
         nc.gpsimd.memset(staged[0:32, :], 0)
-        nc.gpsimd.memset(xt_s[:].bitcast(I32), 0)
         nc.vector.memset(xo_s[:].bitcast(I32), 0)
-        nc.vector.memset(vs_s[:].bitcast(I32), 0)
+        nc.gpsimd.memset(xt_s[:].bitcast(I32), 0)
+        nc.gpsimd.memset(vs_s[:].bitcast(I32), 0)
         for t in range(PACK):
             (nc.vector if t < 2 else nc.gpsimd).memset(hid[t][:], 0.0)
 
@@ -69,58 +68,59 @@ def tile_picked_tokens_plain_two_pairpost_store_plain_kernel(
         sb_t = keep.tile([P, PACK], F32, name="sb_t")
 
         xo_staged = keep.tile([4, M], I32, name="xo_staged")
-        load_staged_rows(xo_staged, 0, xo_scales)
+        load_staged_rows(xo_staged[:], xo_scales[0])
         l2 = load_list("l2", offs2)
-        l4 = load_list("l4", offs4)
-        load_staged_rows(staged, 0, w2_scales)
-        load_staged_rows(staged, 4, w_scales)
         xo_w = load_words("xo_w", xo_words[0].rearrange("p n t -> p (n t)"), M, U32)
+        load_staged_rows(staged[0:4, :], w2_scales[0])
+        load_staged_rows(staged[4:8, :], w_scales[0])
         w2_w = load_words("w2_w", w2_words[0], R, U16)
-        w_w = load_words("w_w", w_words[0].rearrange("p n t -> p (n t)"), R, U32)
-        xt_w = load_words("xt_w", xt_words[0].rearrange("p n t -> p (n t)"), T, U32)
         l1 = load_list("l1", offs)
-        load_scale_rows(xt_s, xt_scales)
+        xt_w = load_words("xt_w", xt_words[0].rearrange("p n t -> p (n t)"), T, U32)
+        l4 = load_list("l4", offs4)
         nc.sync.dma_start(sb_t[:], sb.rearrange("(p t) o -> p (t o)", t=PACK))
+        w_w = load_words("w_w", w_words[0].rearrange("p n t -> p (n t)"), R, U32)
+        load_scale_rows(xt_s, xt_scales, range(4))
         l3 = load_list("l3", offs3)
         nc.sync.dma_start(sa_t[:], sa.rearrange("(p t) o -> p (t o)", t=PACK))
         l5 = load_list("l5", offs5)
         l6 = load_list("l6", offs6)
         vs_w = load_words("vs_w", vs_words[0], V, U16)
-        load_scale_rows(vs_s, vs_scales)
+        load_scale_rows(vs_s, vs_scales, range(4))
 
         xt_gw = held("xt_gw", J, U32)
         xt_gs = held("xt_gs", J, U8)
         xo_gw = held("xo_gw", J, U32)
         xo_gs = held("xo_gs", J, U8)
-        w_dw = keep.tile([P, R], U32, name="w_dw", tag="words", align_bytes=64)
-        dealt_s = keep.tile([P, R], U8, name="dealt_s", tag="planes", align_bytes=64)
+        w_dw = held("w_dw", R, U32)
+        dealt_s = held("dealt_s", R, U8)
         w2_dw = held("w2_dw", R, U16)
         rows_a = [held("a%d" % t, J, F32) for t in range(PACK)]
         rows_b = [held("b%d" % t, J, F32) for t in range(PACK)]
         pick_a = [held("pa%d" % t, S, F32) for t in range(PACK)]
         pick_b = [held("pb%d" % t, S, F32) for t in range(PACK)]
         larger = [held("h%d" % t, S, F32) for t in range(PACK)]
-        hid16 = [held("hid16_%d" % h, PACK * HALF, BF16) for h in range(2)]
-        hq_w = [held("hq_w%d" % h, HALF, U32) for h in range(2)]
-        hq_s = [held("hq_s%d" % h, HALF, U8) for h in range(2)]
+        hid16 = held("hid16", PACK * C, BF16)
+        hq_w = [held("hq_w%d" % q, P, U32) for q in range(4)]
+        hq_s = [held("hq_s%d" % q, P, U8) for q in range(4)]
         halves = [slice(h * HALF, (h + 1) * HALF) for h in range(2)]
         whole = slice(0, J)
 
         def deal_words(dst, src):
             nc.scalar.copy(dst[:].rearrange("p (t m) -> p m t", t=PACK), src[:].rearrange("p (m t) -> p m t", t=PACK))
 
-        def deal_bytes(dst, src):
+        def deal_by_tile(dst, src):
             dealt = dst[:].rearrange("p (t m) -> p t m", t=PACK)
             plain = src.rearrange("p (m t) -> p t m", t=PACK)
             nc.gpsimd.tensor_copy(dealt[:, 0, :], plain[:, 0, :])
             nc.gpsimd.tensor_copy(dealt[:, 1:PACK, :], plain[:, 1:PACK, :])
 
-        def gather_words(dst, src, lst):
-            for h in range(2):
-                nc.vector.tensor_copy(dst[:, halves[h]], src[:].indirect(lst[:, 16 * h : 16 * h + 16]))
+        def gather_half(dst, src, lst, h):
+            nc.vector.tensor_copy(dst[:, halves[h]], src[:].indirect(lst[:, 16 * h : 16 * h + 16]))
 
-        def product(words, first, fmt, picked_words, picked_scales, t, cols):
-            acc = psum.tile([P, J], F32, name="acc")
+        def bank(n):
+            return psum.tile([P, J], F32, name="acc", tag="bank%d" % n)
+
+        def product(acc, words, first, fmt, picked_words, picked_scales, t, cols):
             nc.tensor.matmul_mx(
                 out=acc[:, cols],
                 lhsT=words[:, t * P : (t + 1) * P].bitcast(fmt),
@@ -132,11 +132,11 @@ def tile_picked_tokens_plain_two_pairpost_store_plain_kernel(
             )
             return acc[:, cols]
 
-        def product_a(t, cols):
-            return product(w_dw, 4, FP8X4, xt_gw, xt_gs, t, cols)
+        def product_a(acc, t, cols):
+            return product(acc, w_dw, 4, FP8X4, xt_gw, xt_gs, t, cols)
 
-        def product_b(t, cols):
-            return product(w2_dw, 0, FP4X4, xo_gw, xo_gs, t, cols)
+        def product_b(acc, t, cols):
+            return product(acc, w2_dw, 0, FP4X4, xo_gw, xo_gs, t, cols)
 
         def fetch(dst, rows, lst, scale, t):
             nc.scalar.activation(out=dst[t][:], in_=rows[t][:].indirect(lst[:]), func=COPY, scale=scale[:, t : t + 1])
@@ -145,73 +145,79 @@ def tile_picked_tokens_plain_two_pairpost_store_plain_kernel(
             nc.vector.tensor_tensor(larger[t][:], pick_a[t][:], pick_b[t][:], MAX)
             nc.scalar.activation(out=hid[t][:].indirect(l5[:]), in_=larger[t][:], func=COPY)
 
-        def round_into_slot(t):
-            for h in range(2):
-                nc.vector.tensor_copy(hid16[h][:, t : PACK * HALF : PACK], hid[t][:, halves[h]])
+        def round_into_slot(t, start=0, stop=C):
+            nc.vector.tensor_copy(hid16[:, PACK * start + t : PACK * stop : PACK], hid[t][:, start:stop])
 
         for q in range(4):
             nc.vector.tensor_copy(xo_s[32 * q : 32 * q + 4, :].bitcast(I32), xo_staged[:, q * (M // 4) : (q + 1) * (M // 4)])
+        gather_half(xo_gs, xo_s, l2, 0)
         width = R // 4
         for q in range(1, 4):
             nc.vector.tensor_copy(staged[32 * q : 32 * q + 32, 0:width], staged[0:32, q * width : (q + 1) * width])
-        nc.vector.tensor_copy(xo_gs[:], xo_s[:].indirect(l2[:]))
-        deal_bytes(dealt_s, staged[:, 0:width].bitcast(U8))
+        deal_by_tile(dealt_s, staged[:, 0:width].bitcast(U8))
         deal_words(w2_dw, w2_w)
-        gather_words(xo_gw, xo_w, l2)
-        deal_words(w_dw, w_w)
+        accs = [bank(t) for t in range(3)]
+        for h in range(2):
+            if h == 1:
+                gather_half(xo_gs, xo_s, l2, h)
+            gather_half(xo_gw, xo_w, l2, h)
+            for t in range(3):
+                nc.scalar.activation(out=rows_b[t][:, halves[h]], in_=product_b(accs[t], t, halves[h]), func=COPY)
 
-        for cols in halves:
-            nc.scalar.activation(out=rows_b[0][:, cols], in_=product_b(0, cols), func=COPY)
-        for t in (1, 2):
-            nc.scalar.activation(out=rows_b[t][:], in_=product_b(t, whole), func=COPY)
-        acc_b3 = product_b(3, whole)
-
-        nc.vector.tensor_copy(xt_gs[:], xt_s[:].indirect(l1[:]))
-        gather_words(xt_gw, xt_w, l1)
+        nc.vector.tensor_copy(xt_gw[:], xt_w[:].indirect(l1[:]))
+        deal_by_tile(w_dw, w_w[:])
+        for h in range(2):
+            gather_half(xt_gs, xt_s, l1, h)
         for t in range(3):
             fetch(pick_b, rows_b, l4, sb_t, t)
 
-        for cols in halves:
-            nc.vector.tensor_copy(rows_a[0][:, cols], product_a(0, cols))
+        for h in range(2):
+            nc.vector.tensor_copy(rows_a[0][:, halves[h]], product_a(bank(3 + h), 0, halves[h]))
         fetch(pick_a, rows_a, l3, sa_t, 0)
-        nc.vector.tensor_copy(rows_a[1][:], product_a(1, whole))
+        nc.vector.tensor_copy(rows_a[1][:], product_a(bank(5), 1, whole))
         fetch(pick_a, rows_a, l3, sa_t, 1)
         place(0)
-        nc.vector.tensor_copy(rows_a[2][:], product_a(2, whole))
-        nc.vector.tensor_copy(rows_b[3][:], acc_b3)
+        nc.vector.tensor_copy(rows_a[2][:], product_a(bank(6), 2, whole))
         fetch(pick_a, rows_a, l3, sa_t, 2)
         place(1)
-        nc.vector.tensor_copy(rows_a[3][:], product_a(3, whole))
+        nc.vector.tensor_copy(rows_b[3][:], product_b(bank(3), 3, whole))
+        nc.vector.tensor_copy(rows_a[3][:], product_a(bank(7), 3, whole))
         fetch(pick_b, rows_b, l4, sb_t, 3)
         fetch(pick_a, rows_a, l3, sa_t, 3)
         place(2)
         round_into_slot(0)
         place(3)
-        vs_gw = keep.tile([P, N], U16, name="vs_gw", tag="words", align_bytes=64)
-        vs_gs = keep.tile([P, N], U8, name="vs_gs", tag="planes", align_bytes=64)
+        vs_gw = keep.tile([P, N], U16, name="vs_gw", tag="pa2", align_bytes=64)
+        vs_gs = keep.tile([P, N], U8, name="vs_gs", tag="pb2", align_bytes=64)
         nc.vector.tensor_copy(vs_gs[:], vs_s[:].indirect(l6[:]))
         nc.vector.tensor_copy(vs_gw[:], vs_w[:].indirect(l6[:]))
         round_into_slot(1)
         round_into_slot(2)
-        round_into_slot(3)
 
-        for h in range(2):
-            nc.vector.quantize_mx(out=hq_w[h][:].bitcast(FP8X4), scales=hq_s[h][:], in_=hid16[h][:])
-        for h in range(2):
+        def finish(q):
+            nc.vector.quantize_mx(out=hq_w[q][:].bitcast(FP8X4), scales=hq_s[q][:], in_=hid16[:, PACK * q * P : PACK * (q + 1) * P])
+            acc = bank((0, 1, 2, 4)[q])
             for j in range(2):
-                acc = psum.tile([P, J], F32, name="acc")
                 nc.tensor.matmul_mx(
-                    out=acc[:, 0:HALF],
+                    out=acc[:, j * P : (j + 1) * P],
                     lhsT=vs_gw[:, j * P : (j + 1) * P].bitcast(FP4X4),
                     lhsT_scale=vs_gs[:, j * P : (j + 1) * P],
-                    rhs=hq_w[h][:].bitcast(FP8X4),
-                    rhs_scale=hq_s[h][:],
+                    rhs=hq_w[q][:].bitcast(FP8X4),
+                    rhs_scale=hq_s[q][:],
                     start=True,
                     stop=True,
                 )
-                res = held("res%d%d" % (h, j), HALF, F32)
-                if h == 1 and j == 0:
-                    nc.vector.tensor_copy(res[:], acc[:, 0:HALF])
-                else:
-                    nc.scalar.activation(out=res[:], in_=acc[:, 0:HALF], func=COPY)
-                nc.sync.dma_start(out[j * P : (j + 1) * P, h * HALF : (h + 1) * HALF], res[:])
+            res = held("res%d" % q, N, F32)
+            if q == 3:
+                nc.vector.tensor_copy(res[:], acc[:, 0:N])
+            else:
+                nc.scalar.activation(out=res[:], in_=acc[:, 0:N], func=COPY)
+            nc.sync.dma_start(
+                out[:, q * P : (q + 1) * P].rearrange("(j p) c -> p j c", p=P), res[:].rearrange("p (j c) -> p j c", j=2)
+            )
+
+        round_into_slot(3, 0, P)
+        for q in range(4):
+            if q < 3:
+                round_into_slot(3, (q + 1) * P, (q + 2) * P)
+            finish(q)

@@ -30,8 +30,8 @@ def tile_picked_tokens_plain_two_pairpost_store_plain_kernel(
         keep = ctx.enter_context(tc.tile_pool(name="keep", bufs=1))
         psum = ctx.enter_context(tc.psum_pool(name="psum", bufs=1))
 
-        def held(name, width, dtype):
-            return keep.tile([P, width], dtype, name=name, align_bytes=64)
+        def held(name, width, dtype, after=None):
+            return keep.tile([P, width], dtype, name=name, tag=after or name, align_bytes=64)
 
         def load_list(name, src):
             tile = keep.tile([P, src.shape[1]], U16, name=name)
@@ -43,8 +43,8 @@ def tile_picked_tokens_plain_two_pairpost_store_plain_kernel(
             nc.sync.dma_start(tile[:].bitcast(I32), src.bitcast(I32))
             return tile
 
-        def load_scale_rows(tile, src, quarters):
-            for q in quarters:
+        def load_scale_rows(tile, src):
+            for q in range(4):
                 nc.sync.dma_start(tile[32 * q : 32 * q + 4, :].bitcast(I32), src[0, 4 * q : 4 * q + 4, :].bitcast(I32))
 
         def load_staged_rows(rows, src):
@@ -52,91 +52,125 @@ def tile_picked_tokens_plain_two_pairpost_store_plain_kernel(
                 rows.rearrange("r (q c) -> r q c", q=src.shape[0] // 4), src.bitcast(I32).rearrange("(q r) c -> r q c", r=4)
             )
 
+        def spread_rows(plane, staged, rows):
+            width = staged.shape[1] // 4
+            for q in range(4):
+                nc.vector.tensor_copy(plane[32 * q : 32 * q + rows, :].bitcast(I32), staged[0:rows, q * width : (q + 1) * width])
+
         xt_s = held("xt_s", T, U8)
         xo_s = held("xo_s", M, U8)
         vs_s = held("vs_s", V, U8)
-        staged = held("staged", R, I32)
-        hid = [held("hid%d" % t, C, F32) for t in range(PACK)]
-        nc.gpsimd.memset(staged[0:32, :], 0)
+        w_staged = keep.tile([32, R], I32, name="w_staged", align_bytes=64)
+        hid = [held("hid%d" % t, C, F32) for t in range(2)]
+        nc.gpsimd.memset(w_staged[:], 0)
         nc.vector.memset(xo_s[:].bitcast(I32), 0)
-        nc.gpsimd.memset(xt_s[:].bitcast(I32), 0)
-        nc.gpsimd.memset(vs_s[:].bitcast(I32), 0)
-        for t in range(PACK):
-            (nc.vector if t < 2 else nc.gpsimd).memset(hid[t][:], 0.0)
+        nc.vector.memset(xt_s[:].bitcast(I32), 0)
+        nc.vector.memset(vs_s[:].bitcast(I32), 0)
+        for t in range(2):
+            nc.vector.memset(hid[t][:], 0.0)
 
         sa_t = keep.tile([P, PACK], F32, name="sa_t")
         sb_t = keep.tile([P, PACK], F32, name="sb_t")
 
-        xo_staged = keep.tile([4, M], I32, name="xo_staged")
-        load_staged_rows(xo_staged[:], xo_scales[0])
+        xo_staged = held("xo_staged", M // 2, I32)
+        for u in range(2):
+            load_staged_rows(xo_staged[64 * u : 64 * u + 4, :], xo_scales[0, 8 * u : 8 * u + 8, :])
         l2 = load_list("l2", offs2)
         xo_w = load_words("xo_w", xo_words[0].rearrange("p n t -> p (n t)"), M, U32)
-        load_staged_rows(staged[0:4, :], w2_scales[0])
-        load_staged_rows(staged[4:8, :], w_scales[0])
+        load_staged_rows(w_staged[0:4, :], w2_scales[0])
+        load_staged_rows(w_staged[4:8, :], w_scales[0])
         w2_w = load_words("w2_w", w2_words[0], R, U16)
-        l1 = load_list("l1", offs)
+        w_w = load_words("w_w", w_words[0].rearrange("p n t -> p (n t)"), R, U32)
         xt_w = load_words("xt_w", xt_words[0].rearrange("p n t -> p (n t)"), T, U32)
+        l1 = load_list("l1", offs)
+        load_scale_rows(xt_s, xt_scales)
         l4 = load_list("l4", offs4)
         nc.sync.dma_start(sb_t[:], sb.rearrange("(p t) o -> p (t o)", t=PACK))
-        w_w = load_words("w_w", w_words[0].rearrange("p n t -> p (n t)"), R, U32)
-        load_scale_rows(xt_s, xt_scales, range(4))
         l3 = load_list("l3", offs3)
         nc.sync.dma_start(sa_t[:], sa.rearrange("(p t) o -> p (t o)", t=PACK))
         l5 = load_list("l5", offs5)
         l6 = load_list("l6", offs6)
         vs_w = load_words("vs_w", vs_words[0], V, U16)
-        load_scale_rows(vs_s, vs_scales, range(4))
+        load_scale_rows(vs_s, vs_scales)
 
-        xt_gw = held("xt_gw", J, U32)
-        xt_gs = held("xt_gs", J, U8)
-        xo_gw = held("xo_gw", J, U32)
-        xo_gs = held("xo_gs", J, U8)
-        w_dw = held("w_dw", R, U32)
-        dealt_s = held("dealt_s", R, U8)
-        w2_dw = held("w2_dw", R, U16)
-        rows_a = [held("a%d" % t, J, F32) for t in range(PACK)]
-        rows_b = [held("b%d" % t, J, F32) for t in range(PACK)]
-        pick_a = [held("pa%d" % t, S, F32) for t in range(PACK)]
-        pick_b = [held("pb%d" % t, S, F32) for t in range(PACK)]
-        larger = [held("h%d" % t, S, F32) for t in range(PACK)]
-        hid16 = held("hid16", PACK * C, BF16)
-        hq_w = [held("hq_w%d" % q, P, U32) for q in range(4)]
-        hq_s = [held("hq_s%d" % q, P, U8) for q in range(4)]
         halves = [slice(h * HALF, (h + 1) * HALF) for h in range(2)]
         whole = slice(0, J)
 
-        def deal_words(dst, src):
-            nc.scalar.copy(dst[:].rearrange("p (t m) -> p m t", t=PACK), src[:].rearrange("p (m t) -> p m t", t=PACK))
+        def deal(engine_copy, dst, src, run):
+            engine_copy(
+                dst[:].rearrange("p (t m i) -> p m t i", t=PACK, i=run), src[:].rearrange("p (m i t) -> p m t i", t=PACK, i=run)
+            )
 
-        def deal_by_tile(dst, src):
-            dealt = dst[:].rearrange("p (t m) -> p t m", t=PACK)
-            plain = src.rearrange("p (m t) -> p t m", t=PACK)
-            nc.gpsimd.tensor_copy(dealt[:, 0, :], plain[:, 0, :])
-            nc.gpsimd.tensor_copy(dealt[:, 1:PACK, :], plain[:, 1:PACK, :])
+        def gather(dst, src, offsets):
+            nc.vector.tensor_copy(dst, src[:].indirect(offsets))
 
-        def gather_half(dst, src, lst, h):
-            nc.vector.tensor_copy(dst[:, halves[h]], src[:].indirect(lst[:, 16 * h : 16 * h + 16]))
+        def half_of(lst, h):
+            return lst[:, 16 * h : 16 * h + 16]
 
         def bank(n):
             return psum.tile([P, J], F32, name="acc", tag="bank%d" % n)
 
-        def product(acc, words, first, fmt, picked_words, picked_scales, t, cols):
+        w_s = held("w_s", R, U8)
+        dealt_s = held("dealt_s", R, U8)
+        w_dw = held("w_dw", R, U32)
+        w2_dw = held("w2_dw", R, U16)
+
+        def product(acc, words, first, fmt, t, picked_words, picked_scales):
             nc.tensor.matmul_mx(
-                out=acc[:, cols],
+                out=acc,
                 lhsT=words[:, t * P : (t + 1) * P].bitcast(fmt),
                 lhsT_scale=dealt_s[first:P, t * P : (t + 1) * P],
-                rhs=picked_words[:, cols].bitcast(FP8X4),
-                rhs_scale=picked_scales[:, cols],
+                rhs=picked_words.bitcast(FP8X4),
+                rhs_scale=picked_scales,
                 start=True,
                 stop=True,
             )
-            return acc[:, cols]
+            return acc
+
+        for q in range(4):
+            first, width = 64 * (q // 2), M // 4
+            nc.vector.tensor_copy(
+                xo_s[32 * q : 32 * q + 4, :].bitcast(I32), xo_staged[first : first + 4, (q % 2) * width : (q % 2 + 1) * width]
+            )
+        xo_gs = [held("xo_gs0", HALF, U8)]
+        gather(xo_gs[0][:], xo_s, half_of(l2, 0))
+        spread_rows(w_s, w_staged, 32)
+        deal(nc.vector.tensor_copy, dealt_s, w_s, 16)
+        deal(nc.scalar.copy, w2_dw, w2_w, 8)
+        deal(nc.scalar.copy, w_dw, w_w, 4)
+        xo_gw = [held("xo_gw0", HALF, U32, after="w_staged"), held("xo_gw1", HALF, U32, after="w_s")]
+        xo_gs.append(held("xo_gs1", HALF, U8, after="w2_w"))
+
+        def product_b(acc, t, h):
+            return product(acc[:, halves[h]], w2_dw, 0, FP4X4, t, xo_gw[h][:], xo_gs[h][:])
+
+        rows_b = [held("b%d" % t, J, F32) for t in range(3)]
+        accs = [bank(t) for t in range(3)]
+        gather(xo_gw[0][:], xo_w, half_of(l2, 0))
+        for t in range(3):
+            nc.scalar.activation(out=rows_b[t][:, halves[0]], in_=product_b(accs[t], t, 0), func=COPY)
+        gather(xo_gs[1][:], xo_s, half_of(l2, 1))
+        gather(xo_gw[1][:], xo_w, half_of(l2, 1))
+        for t in range(3):
+            nc.scalar.activation(out=rows_b[t][:, halves[1]], in_=product_b(accs[t], t, 1), func=COPY)
+
+        xt_gw = held("xt_gw", J, U32, after="xo_w")
+        xt_gs = held("xt_gs", J, U8, after="xo_s")
+        gather(xt_gw[:], xt_w, l1[:])
+        for h in range(2):
+            gather(xt_gs[:, halves[h]], xt_s, half_of(l1, h))
+        hid.append(held("hid2", C, F32, after="w_w"))
+        hid.append(held("hid3", C, F32, after="xt_w"))
+        for t in (2, 3):
+            nc.gpsimd.memset(hid[t][:], 0.0)
 
         def product_a(acc, t, cols):
-            return product(acc, w_dw, 4, FP8X4, xt_gw, xt_gs, t, cols)
+            return product(acc[:, cols], w_dw, 4, FP8X4, t, xt_gw[:, cols], xt_gs[:, cols])
 
-        def product_b(acc, t, cols):
-            return product(acc, w2_dw, 0, FP4X4, xo_gw, xo_gs, t, cols)
+        pick_a = [held("pa%d" % t, S, F32) for t in range(PACK)]
+        pick_b = [held("pb%d" % t, S, F32) for t in range(PACK)]
+        larger = [held("h%d" % t, S, F32) for t in range(PACK)]
+        hid16 = held("hid16", PACK * C, BF16)
 
         def fetch(dst, rows, lst, scale, t):
             nc.scalar.activation(out=dst[t][:], in_=rows[t][:].indirect(lst[:]), func=COPY, scale=scale[:, t : t + 1])
@@ -148,62 +182,51 @@ def tile_picked_tokens_plain_two_pairpost_store_plain_kernel(
         def round_into_slot(t, start=0, stop=C):
             nc.vector.tensor_copy(hid16[:, PACK * start + t : PACK * stop : PACK], hid[t][:, start:stop])
 
-        for q in range(4):
-            nc.vector.tensor_copy(xo_s[32 * q : 32 * q + 4, :].bitcast(I32), xo_staged[:, q * (M // 4) : (q + 1) * (M // 4)])
-        gather_half(xo_gs, xo_s, l2, 0)
-        width = R // 4
-        for q in range(1, 4):
-            nc.vector.tensor_copy(staged[32 * q : 32 * q + 32, 0:width], staged[0:32, q * width : (q + 1) * width])
-        deal_by_tile(dealt_s, staged[:, 0:width].bitcast(U8))
-        deal_words(w2_dw, w2_w)
-        accs = [bank(t) for t in range(3)]
-        for h in range(2):
-            if h == 1:
-                gather_half(xo_gs, xo_s, l2, h)
-            gather_half(xo_gw, xo_w, l2, h)
-            for t in range(3):
-                nc.scalar.activation(out=rows_b[t][:, halves[h]], in_=product_b(accs[t], t, halves[h]), func=COPY)
-
-        nc.vector.tensor_copy(xt_gw[:], xt_w[:].indirect(l1[:]))
-        deal_by_tile(w_dw, w_w[:])
-        for h in range(2):
-            gather_half(xt_gs, xt_s, l1, h)
         for t in range(3):
             fetch(pick_b, rows_b, l4, sb_t, t)
 
+        rows_a = [held("a%d" % t, J, F32) for t in range(2)]
         for h in range(2):
             nc.vector.tensor_copy(rows_a[0][:, halves[h]], product_a(bank(3 + h), 0, halves[h]))
         fetch(pick_a, rows_a, l3, sa_t, 0)
         nc.vector.tensor_copy(rows_a[1][:], product_a(bank(5), 1, whole))
         fetch(pick_a, rows_a, l3, sa_t, 1)
         place(0)
+        rows_a.append(held("a2", J, F32, after="pa0"))
         nc.vector.tensor_copy(rows_a[2][:], product_a(bank(6), 2, whole))
         fetch(pick_a, rows_a, l3, sa_t, 2)
         place(1)
-        nc.vector.tensor_copy(rows_b[3][:], product_b(bank(3), 3, whole))
+        rows_b.append(held("b3", J, F32, after="pb0"))
+        acc = bank(3)
+        for h in range(2):
+            product_b(acc, 3, h)
+        nc.vector.tensor_copy(rows_b[3][:], acc[:])
+        rows_a.append(held("a3", J, F32, after="pa1"))
         nc.vector.tensor_copy(rows_a[3][:], product_a(bank(7), 3, whole))
         fetch(pick_b, rows_b, l4, sb_t, 3)
         fetch(pick_a, rows_a, l3, sa_t, 3)
         place(2)
         round_into_slot(0)
         place(3)
-        vs_gw = keep.tile([P, N], U16, name="vs_gw", tag="pa2", align_bytes=64)
-        vs_gs = keep.tile([P, N], U8, name="vs_gs", tag="pb2", align_bytes=64)
-        nc.vector.tensor_copy(vs_gs[:], vs_s[:].indirect(l6[:]))
-        nc.vector.tensor_copy(vs_gw[:], vs_w[:].indirect(l6[:]))
+        vs_gw = held("vs_gw", N, U16, after="pa2")
+        vs_gs = held("vs_gs", N, U8, after="pb2")
+        gather(vs_gs[:], vs_s, l6[:])
+        gather(vs_gw[:], vs_w, l6[:])
         round_into_slot(1)
         round_into_slot(2)
 
         def finish(q):
-            nc.vector.quantize_mx(out=hq_w[q][:].bitcast(FP8X4), scales=hq_s[q][:], in_=hid16[:, PACK * q * P : PACK * (q + 1) * P])
+            hq_w = held("hq_w%d" % q, P, U32)
+            hq_s = held("hq_s%d" % q, P, U8)
+            nc.vector.quantize_mx(out=hq_w[:].bitcast(FP8X4), scales=hq_s[:], in_=hid16[:, PACK * q * P : PACK * (q + 1) * P])
             acc = bank((0, 1, 2, 4)[q])
             for j in range(2):
                 nc.tensor.matmul_mx(
                     out=acc[:, j * P : (j + 1) * P],
                     lhsT=vs_gw[:, j * P : (j + 1) * P].bitcast(FP4X4),
                     lhsT_scale=vs_gs[:, j * P : (j + 1) * P],
-                    rhs=hq_w[q][:].bitcast(FP8X4),
-                    rhs_scale=hq_s[q][:],
+                    rhs=hq_w[:].bitcast(FP8X4),
+                    rhs_scale=hq_s[:],
                     start=True,
                     stop=True,
                 )

@@ -61,13 +61,12 @@ def tile_picked_tokens_plain_two_pairpost_store_plain_kernel(
         xo_s = held("xo_s", M, U8)
         vs_s = held("vs_s", V, U8)
         w_staged = keep.tile([32, R], I32, name="w_staged", align_bytes=64)
-        hid = [held("hid%d" % t, C, F32) for t in range(2)]
-        nc.gpsimd.memset(w_staged[:], 0)
+        hid = [held("hid0", C, F32)]
+        nc.vector.memset(w_staged[:], 0)
         nc.vector.memset(xo_s[:].bitcast(I32), 0)
-        nc.vector.memset(xt_s[:].bitcast(I32), 0)
-        nc.vector.memset(vs_s[:].bitcast(I32), 0)
-        for t in range(2):
-            nc.vector.memset(hid[t][:], 0.0)
+        nc.gpsimd.memset(xt_s[:].bitcast(I32), 0)
+        nc.gpsimd.memset(hid[0][:], 0.0)
+        nc.gpsimd.memset(vs_s[:].bitcast(I32), 0)
 
         sa_t = keep.tile([P, PACK], F32, name="sa_t")
         sb_t = keep.tile([P, PACK], F32, name="sb_t")
@@ -76,9 +75,9 @@ def tile_picked_tokens_plain_two_pairpost_store_plain_kernel(
         for u in range(2):
             load_staged_rows(xo_staged[64 * u : 64 * u + 4, :], xo_scales[0, 8 * u : 8 * u + 8, :])
         l2 = load_list("l2", offs2)
-        xo_w = load_words("xo_w", xo_words[0].rearrange("p n t -> p (n t)"), M, U32)
         load_staged_rows(w_staged[0:4, :], w2_scales[0])
         load_staged_rows(w_staged[4:8, :], w_scales[0])
+        xo_w = load_words("xo_w", xo_words[0].rearrange("p n t -> p (n t)"), M, U32)
         w2_w = load_words("w2_w", w2_words[0], R, U16)
         w_w = load_words("w_w", w_words[0].rearrange("p n t -> p (n t)"), R, U32)
         xt_w = load_words("xt_w", xt_words[0].rearrange("p n t -> p (n t)"), T, U32)
@@ -159,10 +158,6 @@ def tile_picked_tokens_plain_two_pairpost_store_plain_kernel(
         gather(xt_gw[:], xt_w, l1[:])
         for h in range(2):
             gather(xt_gs[:, halves[h]], xt_s, half_of(l1, h))
-        hid.append(held("hid2", C, F32, after="w_w"))
-        hid.append(held("hid3", C, F32, after="xt_w"))
-        for t in (2, 3):
-            nc.gpsimd.memset(hid[t][:], 0.0)
 
         def product_a(acc, t, cols):
             return product(acc[:, cols], w_dw, 4, FP8X4, t, xt_gw[:, cols], xt_gs[:, cols])
@@ -195,6 +190,8 @@ def tile_picked_tokens_plain_two_pairpost_store_plain_kernel(
         rows_a.append(held("a2", J, F32, after="pa0"))
         nc.vector.tensor_copy(rows_a[2][:], product_a(bank(6), 2, whole))
         fetch(pick_a, rows_a, l3, sa_t, 2)
+        hid.append(held("hid1", C, F32, after="a1"))
+        nc.vector.memset(hid[1][:], 0.0)
         place(1)
         rows_b.append(held("b3", J, F32, after="pb0"))
         acc = bank(3)
@@ -205,8 +202,12 @@ def tile_picked_tokens_plain_two_pairpost_store_plain_kernel(
         nc.vector.tensor_copy(rows_a[3][:], product_a(bank(7), 3, whole))
         fetch(pick_b, rows_b, l4, sb_t, 3)
         fetch(pick_a, rows_a, l3, sa_t, 3)
+        hid.append(held("hid2", C, F32, after="pa0"))
+        nc.vector.memset(hid[2][:], 0.0)
         place(2)
         round_into_slot(0)
+        hid.append(held("hid3", C, F32, after="pb0"))
+        nc.vector.memset(hid[3][:], 0.0)
         place(3)
         vs_gw = held("vs_gw", N, U16, after="pa2")
         vs_gs = held("vs_gs", N, U8, after="pb2")
@@ -219,8 +220,12 @@ def tile_picked_tokens_plain_two_pairpost_store_plain_kernel(
             hq_w = held("hq_w%d" % q, P, U32)
             hq_s = held("hq_s%d" % q, P, U8)
             nc.vector.quantize_mx(out=hq_w[:].bitcast(FP8X4), scales=hq_s[:], in_=hid16[:, PACK * q * P : PACK * (q + 1) * P])
-            acc = bank((0, 1, 2, 4)[q])
+            cols = slice(q * P, (q + 1) * P)
+            last = q == 3
+            acc = bank(q)
             for j in range(2):
+                if last and j == 1:
+                    acc = bank(4)
                 nc.tensor.matmul_mx(
                     out=acc[:, j * P : (j + 1) * P],
                     lhsT=vs_gw[:, j * P : (j + 1) * P].bitcast(FP4X4),
@@ -230,14 +235,18 @@ def tile_picked_tokens_plain_two_pairpost_store_plain_kernel(
                     start=True,
                     stop=True,
                 )
-            res = held("res%d" % q, N, F32)
-            if q == 3:
-                nc.vector.tensor_copy(res[:], acc[:, 0:N])
-            else:
+                if last:
+                    res = held("res3%d" % j, P, F32)
+                    if j == 0:
+                        nc.vector.tensor_copy(res[:], acc[:, 0:P])
+                        nc.sync.dma_start(out[0:P, cols], res[:])
+                    else:
+                        nc.scalar.activation(out=res[:], in_=acc[:, P:N], func=COPY)
+                        nc.scalar.dma_start(out[P:N, cols], res[:])
+            if not last:
+                res = held("res%d" % q, N, F32)
                 nc.scalar.activation(out=res[:], in_=acc[:, 0:N], func=COPY)
-            nc.sync.dma_start(
-                out[:, q * P : (q + 1) * P].rearrange("(j p) c -> p j c", p=P), res[:].rearrange("p (j c) -> p j c", j=2)
-            )
+                nc.sync.dma_start(out[:, cols].rearrange("(j p) c -> p j c", p=P), res[:].rearrange("p (j c) -> p j c", j=2))
 
         round_into_slot(3, 0, P)
         for q in range(4):

@@ -13,12 +13,15 @@ FP4X4 = mybir.dt.float4_e2m1fn_x4
 COPY = mybir.ActivationFunctionType.Copy
 MAX = mybir.AluOpType.max
 
+K, J, R, T, Z, M, S, C, N, V = 512, 512, 512, 1024, 512, 1024, 256, 512, 256, 1024
 P = 128
 PACK = 4
-J, R, T, M, S, C, N, V = 512, 512, 1024, 1024, 256, 512, 256, 1024
-HALF = 256
+QUADS = 4
+HALF = J // 2
+LINE = 16
+W2_FIRST, W_FIRST = 0, 4
 
-FLOPS = 2 * 512 * R * J * 2 + 2 * R * N * C
+FLOPS = 2 * K * R * J + 2 * Z * R * J + 2 * R * N * C
 
 
 def tile_picked_tokens_plain_two_pairpost_store_plain_kernel(
@@ -33,6 +36,9 @@ def tile_picked_tokens_plain_two_pairpost_store_plain_kernel(
         def held(name, width, dtype, after=None):
             return keep.tile([P, width], dtype, name=name, tag=after or name, align_bytes=64)
 
+        def bank(n):
+            return psum.tile([P, J], F32, name="acc", tag="bank%d" % n)
+
         def load_list(name, src):
             tile = keep.tile([P, src.shape[1]], U16, name=name)
             nc.sync.dma_start(tile[:], src)
@@ -44,56 +50,13 @@ def tile_picked_tokens_plain_two_pairpost_store_plain_kernel(
             return tile
 
         def load_scale_rows(tile, src):
-            for q in range(4):
+            for q in range(QUADS):
                 nc.sync.dma_start(tile[32 * q : 32 * q + 4, :].bitcast(I32), src[0, 4 * q : 4 * q + 4, :].bitcast(I32))
 
         def load_staged_rows(rows, src):
             nc.sync.dma_start(
-                rows.rearrange("r (q c) -> r q c", q=src.shape[0] // 4), src.bitcast(I32).rearrange("(q r) c -> r q c", r=4)
+                rows.rearrange("i (q c) -> i q c", q=src.shape[0] // 4), src.bitcast(I32).rearrange("(q i) c -> i q c", i=4)
             )
-
-        def spread_rows(plane, staged, rows):
-            width = staged.shape[1] // 4
-            for q in range(4):
-                nc.vector.tensor_copy(plane[32 * q : 32 * q + rows, :].bitcast(I32), staged[0:rows, q * width : (q + 1) * width])
-
-        xt_s = held("xt_s", T, U8)
-        xo_s = held("xo_s", M, U8)
-        vs_s = held("vs_s", V, U8)
-        w_staged = keep.tile([32, R], I32, name="w_staged", align_bytes=64)
-        hid = [held("hid0", C, F32)]
-        nc.vector.memset(w_staged[:], 0)
-        nc.vector.memset(xo_s[:].bitcast(I32), 0)
-        nc.gpsimd.memset(xt_s[:].bitcast(I32), 0)
-        nc.gpsimd.memset(hid[0][:], 0.0)
-        nc.gpsimd.memset(vs_s[:].bitcast(I32), 0)
-
-        sa_t = keep.tile([P, PACK], F32, name="sa_t")
-        sb_t = keep.tile([P, PACK], F32, name="sb_t")
-
-        xo_staged = held("xo_staged", M // 2, I32)
-        for u in range(2):
-            load_staged_rows(xo_staged[64 * u : 64 * u + 4, :], xo_scales[0, 8 * u : 8 * u + 8, :])
-        l2 = load_list("l2", offs2)
-        load_staged_rows(w_staged[0:4, :], w2_scales[0])
-        load_staged_rows(w_staged[4:8, :], w_scales[0])
-        xo_w = load_words("xo_w", xo_words[0].rearrange("p n t -> p (n t)"), M, U32)
-        w2_w = load_words("w2_w", w2_words[0], R, U16)
-        w_w = load_words("w_w", w_words[0].rearrange("p n t -> p (n t)"), R, U32)
-        xt_w = load_words("xt_w", xt_words[0].rearrange("p n t -> p (n t)"), T, U32)
-        l1 = load_list("l1", offs)
-        load_scale_rows(xt_s, xt_scales)
-        l4 = load_list("l4", offs4)
-        nc.sync.dma_start(sb_t[:], sb.rearrange("(p t) o -> p (t o)", t=PACK))
-        l3 = load_list("l3", offs3)
-        nc.sync.dma_start(sa_t[:], sa.rearrange("(p t) o -> p (t o)", t=PACK))
-        l5 = load_list("l5", offs5)
-        l6 = load_list("l6", offs6)
-        vs_w = load_words("vs_w", vs_words[0], V, U16)
-        load_scale_rows(vs_s, vs_scales)
-
-        halves = [slice(h * HALF, (h + 1) * HALF) for h in range(2)]
-        whole = slice(0, J)
 
         def deal(engine_copy, dst, src, run):
             engine_copy(
@@ -104,10 +67,42 @@ def tile_picked_tokens_plain_two_pairpost_store_plain_kernel(
             nc.vector.tensor_copy(dst, src[:].indirect(offsets))
 
         def half_of(lst, h):
-            return lst[:, 16 * h : 16 * h + 16]
+            return lst[:, h * (HALF // 16) : (h + 1) * (HALF // 16)]
 
-        def bank(n):
-            return psum.tile([P, J], F32, name="acc", tag="bank%d" % n)
+        halves = [slice(h * HALF, (h + 1) * HALF) for h in range(2)]
+        whole = slice(0, J)
+
+        xt_s = held("xt_s", T, U8)
+        xo_s = held("xo_s", M, U8)
+        w_staged = keep.tile([32, R], I32, name="w_staged", align_bytes=64)
+        hid = [held("hid0", C, F32)]
+        nc.vector.memset(w_staged[:], 0)
+        nc.vector.memset(xo_s[:].bitcast(I32), 0)
+        nc.vector.memset(xt_s[:].bitcast(I32), 0)
+        nc.vector.memset(hid[0][:], 0.0)
+
+        sa_t = keep.tile([P, PACK], F32, name="sa_t")
+        sb_t = keep.tile([P, PACK], F32, name="sb_t")
+
+        xo_staged = held("xo_staged", M // 2, I32)
+        for u in range(2):
+            load_staged_rows(xo_staged[64 * u : 64 * u + 4, :], xo_scales[0, 8 * u : 8 * u + 8, :])
+        idx2 = load_list("idx2", offs2)
+        load_staged_rows(w_staged[W2_FIRST : W2_FIRST + 4, :], w2_scales[0])
+        load_staged_rows(w_staged[W_FIRST : W_FIRST + 4, :], w_scales[0])
+        xo_w = load_words("xo_w", xo_words[0].rearrange("p n t -> p (n t)"), M, U32)
+        w2_w = load_words("w2_w", w2_words[0], R, U16)
+        w_w = load_words("w_w", w_words[0].rearrange("p n t -> p (n t)"), R, U32)
+        xt_w = load_words("xt_w", xt_words[0].rearrange("p n t -> p (n t)"), T, U32)
+        idx = load_list("idx", offs)
+        load_scale_rows(xt_s, xt_scales)
+        idx4 = load_list("idx4", offs4)
+        nc.sync.dma_start(sb_t[:], sb.rearrange("(p t) o -> p (t o)", t=PACK))
+        idx3 = load_list("idx3", offs3)
+        nc.sync.dma_start(sa_t[:], sa.rearrange("(p t) o -> p (t o)", t=PACK))
+        idx5 = load_list("idx5", offs5)
+        idx6 = load_list("idx6", offs6)
+        vs_w = load_words("vs_w", vs_words[0], V, U16)
 
         w_s = held("w_s", R, U8)
         dealt_s = held("dealt_s", R, U8)
@@ -126,106 +121,118 @@ def tile_picked_tokens_plain_two_pairpost_store_plain_kernel(
             )
             return acc
 
-        for q in range(4):
-            first, width = 64 * (q // 2), M // 4
+        for q in range(QUADS):
+            staged_at, row_words = 64 * (q // 2), M // 4
             nc.vector.tensor_copy(
-                xo_s[32 * q : 32 * q + 4, :].bitcast(I32), xo_staged[first : first + 4, (q % 2) * width : (q % 2 + 1) * width]
+                xo_s[32 * q : 32 * q + 4, :].bitcast(I32),
+                xo_staged[staged_at : staged_at + 4, (q % 2) * row_words : (q % 2 + 1) * row_words],
             )
         xo_gs = [held("xo_gs0", HALF, U8)]
-        gather(xo_gs[0][:], xo_s, half_of(l2, 0))
-        spread_rows(w_s, w_staged, 32)
-        deal(nc.vector.tensor_copy, dealt_s, w_s, 16)
-        deal(nc.scalar.copy, w2_dw, w2_w, 8)
-        deal(nc.scalar.copy, w_dw, w_w, 4)
+        gather(xo_gs[0][:], xo_s, half_of(idx2, 0))
+        for q in range(QUADS):
+            row_words = R // 4
+            nc.vector.tensor_copy(w_s[32 * q : 32 * q + 32, :].bitcast(I32), w_staged[0:32, q * row_words : (q + 1) * row_words])
+        deal(nc.vector.tensor_copy, dealt_s, w_s, LINE)
+        deal(nc.scalar.copy, w2_dw, w2_w, LINE // 2)
+        deal(nc.scalar.copy, w_dw, w_w, LINE // 4)
         xo_gw = [held("xo_gw0", HALF, U32, after="w_staged"), held("xo_gw1", HALF, U32, after="w_s")]
         xo_gs.append(held("xo_gs1", HALF, U8, after="w2_w"))
 
         def product_b(acc, t, h):
-            return product(acc[:, halves[h]], w2_dw, 0, FP4X4, t, xo_gw[h][:], xo_gs[h][:])
+            return product(acc[:, halves[h]], w2_dw, W2_FIRST, FP4X4, t, xo_gw[h][:], xo_gs[h][:])
 
-        rows_b = [held("b%d" % t, J, F32) for t in range(3)]
-        accs = [bank(t) for t in range(3)]
-        gather(xo_gw[0][:], xo_w, half_of(l2, 0))
-        for t in range(3):
+        early = range(PACK - 1)
+        rows_b = [held("b%d" % t, J, F32) for t in early]
+        accs = [bank(t) for t in early]
+        gather(xo_gw[0][:], xo_w, half_of(idx2, 0))
+        for t in early:
             nc.scalar.activation(out=rows_b[t][:, halves[0]], in_=product_b(accs[t], t, 0), func=COPY)
-        gather(xo_gs[1][:], xo_s, half_of(l2, 1))
-        gather(xo_gw[1][:], xo_w, half_of(l2, 1))
-        for t in range(3):
+        gather(xo_gs[1][:], xo_s, half_of(idx2, 1))
+        gather(xo_gw[1][:], xo_w, half_of(idx2, 1))
+        for t in early:
             nc.scalar.activation(out=rows_b[t][:, halves[1]], in_=product_b(accs[t], t, 1), func=COPY)
 
         xt_gw = held("xt_gw", J, U32, after="xo_w")
         xt_gs = held("xt_gs", J, U8, after="xo_s")
-        gather(xt_gw[:], xt_w, l1[:])
+        gather(xt_gw[:], xt_w, idx[:])
         for h in range(2):
-            gather(xt_gs[:, halves[h]], xt_s, half_of(l1, h))
+            gather(xt_gs[:, halves[h]], xt_s, half_of(idx, h))
+        vs_s = held("vs_s", V, U8, after="xt_s")
+        nc.gpsimd.memset(vs_s[:].bitcast(I32), 0)
+        load_scale_rows(vs_s, vs_scales)
 
         def product_a(acc, t, cols):
-            return product(acc[:, cols], w_dw, 4, FP8X4, t, xt_gw[:, cols], xt_gs[:, cols])
+            return product(acc[:, cols], w_dw, W_FIRST, FP8X4, t, xt_gw[:, cols], xt_gs[:, cols])
 
-        pick_a = [held("pa%d" % t, S, F32) for t in range(PACK)]
-        pick_b = [held("pb%d" % t, S, F32) for t in range(PACK)]
-        larger = [held("h%d" % t, S, F32) for t in range(PACK)]
+        pick_a = [held("pick_a%d" % t, S, F32) for t in range(PACK)]
+        pick_b = [held("pick_b%d" % t, S, F32) for t in range(PACK)]
+        larger = [held("larger%d" % t, S, F32) for t in range(PACK)]
         hid16 = held("hid16", PACK * C, BF16)
 
-        def fetch(dst, rows, lst, scale, t):
-            nc.scalar.activation(out=dst[t][:], in_=rows[t][:].indirect(lst[:]), func=COPY, scale=scale[:, t : t + 1])
+        def fetch(dst, rows, lst, weight, t):
+            nc.scalar.activation(out=dst[t][:], in_=rows[t][:].indirect(lst[:]), func=COPY, scale=weight[:, t : t + 1])
 
         def place(t):
             nc.vector.tensor_tensor(larger[t][:], pick_a[t][:], pick_b[t][:], MAX)
-            nc.scalar.activation(out=hid[t][:].indirect(l5[:]), in_=larger[t][:], func=COPY)
+            nc.scalar.activation(out=hid[t][:].indirect(idx5[:]), in_=larger[t][:], func=COPY)
 
-        def round_into_slot(t, start=0, stop=C):
+        def cleared_page(t, after):
+            hid.append(held("hid%d" % t, C, F32, after=after))
+            nc.gpsimd.memset(hid[t][:], 0.0)
+
+        def round_into_hid16(t, start=0, stop=C):
             nc.vector.tensor_copy(hid16[:, PACK * start + t : PACK * stop : PACK], hid[t][:, start:stop])
 
-        for t in range(3):
-            fetch(pick_b, rows_b, l4, sb_t, t)
+        for t in early:
+            fetch(pick_b, rows_b, idx4, sb_t, t)
 
         rows_a = [held("a%d" % t, J, F32) for t in range(2)]
         for h in range(2):
             nc.vector.tensor_copy(rows_a[0][:, halves[h]], product_a(bank(3 + h), 0, halves[h]))
-        fetch(pick_a, rows_a, l3, sa_t, 0)
+        fetch(pick_a, rows_a, idx3, sa_t, 0)
         nc.vector.tensor_copy(rows_a[1][:], product_a(bank(5), 1, whole))
-        fetch(pick_a, rows_a, l3, sa_t, 1)
+        fetch(pick_a, rows_a, idx3, sa_t, 1)
         place(0)
-        rows_a.append(held("a2", J, F32, after="pa0"))
+        rows_a.append(held("a2", J, F32, after="pick_a0"))
         nc.vector.tensor_copy(rows_a[2][:], product_a(bank(6), 2, whole))
-        fetch(pick_a, rows_a, l3, sa_t, 2)
-        hid.append(held("hid1", C, F32, after="a1"))
-        nc.vector.memset(hid[1][:], 0.0)
+        fetch(pick_a, rows_a, idx3, sa_t, 2)
+        cleared_page(1, after="a1")
         place(1)
-        rows_b.append(held("b3", J, F32, after="pb0"))
-        acc = bank(3)
+        rows_b.append(held("b3", J, F32, after="pick_b0"))
+        acc_b3 = bank(3)
         for h in range(2):
-            product_b(acc, 3, h)
-        nc.vector.tensor_copy(rows_b[3][:], acc[:])
-        rows_a.append(held("a3", J, F32, after="pa1"))
+            product_b(acc_b3, 3, h)
+        nc.vector.tensor_copy(rows_b[3][:], acc_b3[:])
+        rows_a.append(held("a3", J, F32, after="pick_a1"))
         nc.vector.tensor_copy(rows_a[3][:], product_a(bank(7), 3, whole))
-        fetch(pick_b, rows_b, l4, sb_t, 3)
-        fetch(pick_a, rows_a, l3, sa_t, 3)
-        hid.append(held("hid2", C, F32, after="pa0"))
-        nc.vector.memset(hid[2][:], 0.0)
+        fetch(pick_b, rows_b, idx4, sb_t, 3)
+        fetch(pick_a, rows_a, idx3, sa_t, 3)
+        cleared_page(2, after="a0")
+        vs_gw = held("vs_gw", N, U16, after="pick_b1")
+        vs_gs = held("vs_gs", N, U8, after="larger0")
+        gather(vs_gw[:], vs_w, idx6[:])
+        gather(vs_gs[:], vs_s, idx6[:])
+        round_into_hid16(0)
         place(2)
-        round_into_slot(0)
-        hid.append(held("hid3", C, F32, after="pb0"))
-        nc.vector.memset(hid[3][:], 0.0)
+        cleared_page(3, after="xo_w")
         place(3)
-        vs_gw = held("vs_gw", N, U16, after="pa2")
-        vs_gs = held("vs_gs", N, U8, after="pb2")
-        gather(vs_gs[:], vs_s, l6[:])
-        gather(vs_gw[:], vs_w, l6[:])
-        round_into_slot(1)
-        round_into_slot(2)
+        round_into_hid16(1)
+        round_into_hid16(2)
 
-        def finish(q):
-            hq_w = held("hq_w%d" % q, P, U32)
-            hq_s = held("hq_s%d" % q, P, U8)
-            nc.vector.quantize_mx(out=hq_w[:].bitcast(FP8X4), scales=hq_s[:], in_=hid16[:, PACK * q * P : PACK * (q + 1) * P])
-            cols = slice(q * P, (q + 1) * P)
-            last = q == 3
-            acc = bank(q)
-            for j in range(2):
+        pieces = C // P
+
+        def finish(piece):
+            hq_w = held("hq_w%d" % piece, P, U32)
+            hq_s = held("hq_s%d" % piece, P, U8)
+            nc.vector.quantize_mx(
+                out=hq_w[:].bitcast(FP8X4), scales=hq_s[:], in_=hid16[:, PACK * piece * P : PACK * (piece + 1) * P]
+            )
+            cols = slice(piece * P, (piece + 1) * P)
+            last = piece == pieces - 1
+            acc = bank(piece)
+            for j in range(N // P):
                 if last and j == 1:
-                    acc = bank(4)
+                    acc = bank(pieces)
                 nc.tensor.matmul_mx(
                     out=acc[:, j * P : (j + 1) * P],
                     lhsT=vs_gw[:, j * P : (j + 1) * P].bitcast(FP4X4),
@@ -236,20 +243,20 @@ def tile_picked_tokens_plain_two_pairpost_store_plain_kernel(
                     stop=True,
                 )
                 if last:
-                    res = held("res3%d" % j, P, F32)
+                    res = held("res_last%d" % j, P, F32)
                     if j == 0:
                         nc.vector.tensor_copy(res[:], acc[:, 0:P])
                         nc.sync.dma_start(out[0:P, cols], res[:])
                     else:
                         nc.scalar.activation(out=res[:], in_=acc[:, P:N], func=COPY)
-                        nc.scalar.dma_start(out[P:N, cols], res[:])
+                        nc.sync.dma_start(out[P:N, cols], res[:])
             if not last:
-                res = held("res%d" % q, N, F32)
+                res = held("res%d" % piece, N, F32)
                 nc.scalar.activation(out=res[:], in_=acc[:, 0:N], func=COPY)
                 nc.sync.dma_start(out[:, cols].rearrange("(j p) c -> p j c", p=P), res[:].rearrange("p (j c) -> p j c", j=2))
 
-        round_into_slot(3, 0, P)
-        for q in range(4):
-            if q < 3:
-                round_into_slot(3, (q + 1) * P, (q + 2) * P)
-            finish(q)
+        round_into_hid16(PACK - 1, 0, P)
+        for piece in range(pieces):
+            if piece + 1 < pieces:
+                round_into_hid16(PACK - 1, (piece + 1) * P, (piece + 2) * P)
+            finish(piece)

from contextlib import ExitStack

import concourse.mybir as mybir

F32 = mybir.dt.float32
BF16 = mybir.dt.bfloat16
I32 = mybir.dt.int32
U32 = mybir.dt.uint32
U16 = mybir.dt.uint16
U8 = mybir.dt.uint8
FP8X4 = mybir.dt.float8_e4m3fn_x4
FP4X4 = mybir.dt.float4_e2m1fn_x4
COPY = mybir.ActivationFunctionType.Copy
MAX = mybir.AluOpType.max

K, J, R, T, Z, M, S, C, N, V = 512, 512, 512, 1024, 512, 1024, 256, 512, 256, 1024
P = 128
PACK = 4
QUADS = 4
HALF = J // 2
LINE = 16
W2_FIRST, W_FIRST = 0, 4

FLOPS = 2 * K * R * J + 2 * Z * R * J + 2 * R * N * C


def tile_picked_tokens_plain_two_pairpost_store_plain_kernel(
    tc, xt_words, xt_scales, w_words, w_scales, xo_words, xo_scales, w2_words, w2_scales, sa, sb,
    vs_words, vs_scales, offs, offs2, offs3, offs4, offs5, offs6, out,
):
    nc = tc.nc
    with ExitStack() as ctx:
        keep = ctx.enter_context(tc.tile_pool(name="keep", bufs=1))
        psum = ctx.enter_context(tc.psum_pool(name="psum", bufs=1))

        def held(name, width, dtype, after=None):
            return keep.tile([P, width], dtype, name=name, tag=after or name, align_bytes=64)

        def bank(n):
            return psum.tile([P, J], F32, name="acc", tag="bank%d" % n)

        def load_list(name, src):
            tile = keep.tile([P, src.shape[1]], U16, name=name)
            nc.sync.dma_start(tile[:], src)
            return tile

        def load_words(name, src, width, dtype):
            tile = held(name, width, dtype)
            nc.sync.dma_start(tile[:].bitcast(I32), src.bitcast(I32))
            return tile

        def load_scale_rows(tile, src):
            for q in range(QUADS):
                nc.sync.dma_start(tile[32 * q : 32 * q + 4, :].bitcast(I32), src[0, 4 * q : 4 * q + 4, :].bitcast(I32))

        def load_staged_rows(rows, src):
            nc.sync.dma_start(
                rows.rearrange("i (q c) -> i q c", q=src.shape[0] // 4), src.bitcast(I32).rearrange("(q i) c -> i q c", i=4)
            )

        def deal(engine_copy, dst, src, run):
            engine_copy(
                dst[:].rearrange("p (t m i) -> p m t i", t=PACK, i=run), src[:].rearrange("p (m i t) -> p m t i", t=PACK, i=run)
            )

        def gather(dst, src, offsets):
            nc.vector.tensor_copy(dst, src[:].indirect(offsets))

        def half_of(lst, h):
            return lst[:, h * (HALF // 16) : (h + 1) * (HALF // 16)]

        halves = [slice(h * HALF, (h + 1) * HALF) for h in range(2)]
        whole = slice(0, J)

        xt_s = held("xt_s", T, U8)
        xo_s = held("xo_s", M, U8)
        w_staged = keep.tile([32, R], I32, name="w_staged", align_bytes=64)
        hid = [held("hid0", C, F32)]
        nc.vector.memset(w_staged[:], 0)
        nc.vector.memset(xo_s[:].bitcast(I32), 0)
        nc.vector.memset(xt_s[:].bitcast(I32), 0)
        nc.vector.memset(hid[0][:], 0.0)

        sa_t = keep.tile([P, PACK], F32, name="sa_t")
        sb_t = keep.tile([P, PACK], F32, name="sb_t")

        xo_staged = held("xo_staged", M // 2, I32)
        for u in range(2):
            load_staged_rows(xo_staged[64 * u : 64 * u + 4, :], xo_scales[0, 8 * u : 8 * u + 8, :])
        idx2 = load_list("idx2", offs2)
        load_staged_rows(w_staged[W2_FIRST : W2_FIRST + 4, :], w2_scales[0])
        load_staged_rows(w_staged[W_FIRST : W_FIRST + 4, :], w_scales[0])
        xo_w = load_words("xo_w", xo_words[0].rearrange("p n t -> p (n t)"), M, U32)
        w2_w = load_words("w2_w", w2_words[0], R, U16)
        w_w = load_words("w_w", w_words[0].rearrange("p n t -> p (n t)"), R, U32)
        xt_w = load_words("xt_w", xt_words[0].rearrange("p n t -> p (n t)"), T, U32)
        idx = load_list("idx", offs)
        load_scale_rows(xt_s, xt_scales)
        idx4 = load_list("idx4", offs4)
        nc.sync.dma_start(sb_t[:], sb.rearrange("(p t) o -> p (t o)", t=PACK))
        idx3 = load_list("idx3", offs3)
        nc.sync.dma_start(sa_t[:], sa.rearrange("(p t) o -> p (t o)", t=PACK))
        idx5 = load_list("idx5", offs5)
        idx6 = load_list("idx6", offs6)
        vs_w = load_words("vs_w", vs_words[0], V, U16)

        w_s = held("w_s", R, U8)
        dealt_s = held("dealt_s", R, U8)
        w_dw = held("w_dw", R, U32)
        w2_dw = held("w2_dw", R, U16)

        def product(acc, words, first, fmt, t, picked_words, picked_scales):
            nc.tensor.matmul_mx(
                out=acc,
                lhsT=words[:, t * P : (t + 1) * P].bitcast(fmt),
                lhsT_scale=dealt_s[first:P, t * P : (t + 1) * P],
                rhs=picked_words.bitcast(FP8X4),
                rhs_scale=picked_scales,
                start=True,
                stop=True,
            )
            return acc

        for q in range(QUADS):
            staged_at, row_words = 64 * (q // 2), M // 4
            nc.vector.tensor_copy(
                xo_s[32 * q : 32 * q + 4, :].bitcast(I32),
                xo_staged[staged_at : staged_at + 4, (q % 2) * row_words : (q % 2 + 1) * row_words],
            )
        xo_gs = [held("xo_gs0", HALF, U8)]
        gather(xo_gs[0][:], xo_s, half_of(idx2, 0))
        for q in range(QUADS):
            row_words = R // 4
            nc.vector.tensor_copy(w_s[32 * q : 32 * q + 32, :].bitcast(I32), w_staged[0:32, q * row_words : (q + 1) * row_words])
        deal(nc.vector.tensor_copy, dealt_s, w_s, LINE)
        deal(nc.scalar.copy, w2_dw, w2_w, LINE // 2)
        deal(nc.scalar.copy, w_dw, w_w, LINE // 4)
        xo_gw = [held("xo_gw0", HALF, U32, after="w_staged"), held("xo_gw1", HALF, U32, after="w_s")]
        xo_gs.append(held("xo_gs1", HALF, U8, after="w2_w"))

        def product_b(acc, t, h):
            return product(acc[:, halves[h]], w2_dw, W2_FIRST, FP4X4, t, xo_gw[h][:], xo_gs[h][:])

        early = range(PACK - 1)
        rows_b = [held("b%d" % t, J, F32) for t in early]
        accs = [bank(t) for t in early]
        gather(xo_gw[0][:], xo_w, half_of(idx2, 0))
        for t in early:
            nc.scalar.activation(out=rows_b[t][:, halves[0]], in_=product_b(accs[t], t, 0), func=COPY)
        gather(xo_gs[1][:], xo_s, half_of(idx2, 1))
        gather(xo_gw[1][:], xo_w, half_of(idx2, 1))
        for t in early:
            nc.scalar.activation(out=rows_b[t][:, halves[1]], in_=product_b(accs[t], t, 1), func=COPY)

        xt_gw = held("xt_gw", J, U32, after="xo_w")
        xt_gs = held("xt_gs", J, U8, after="xo_s")
        gather(xt_gw[:], xt_w, idx[:])
        for h in range(2):
            gather(xt_gs[:, halves[h]], xt_s, half_of(idx, h))
        vs_s = held("vs_s", V, U8, after="xt_s")
        nc.gpsimd.memset(vs_s[:].bitcast(I32), 0)
        load_scale_rows(vs_s, vs_scales)

        def product_a(acc, t, cols):
            return product(acc[:, cols], w_dw, W_FIRST, FP8X4, t, xt_gw[:, cols], xt_gs[:, cols])

        pick_a = [held("pick_a%d" % t, S, F32) for t in range(PACK)]
        pick_b = [held("pick_b%d" % t, S, F32) for t in range(PACK)]
        larger = [held("larger%d" % t, S, F32) for t in range(PACK)]
        hid16 = held("hid16", PACK * C, BF16)

        def fetch(dst, rows, lst, weight, t):
            nc.scalar.activation(out=dst[t][:], in_=rows[t][:].indirect(lst[:]), func=COPY, scale=weight[:, t : t + 1])

        def place(t):
            nc.vector.tensor_tensor(larger[t][:], pick_a[t][:], pick_b[t][:], MAX)
            nc.scalar.activation(out=hid[t][:].indirect(idx5[:]), in_=larger[t][:], func=COPY)

        def cleared_page(t, after):
            hid.append(held("hid%d" % t, C, F32, after=after))
            nc.gpsimd.memset(hid[t][:], 0.0)

        def round_into_hid16(t, start=0, stop=C):
            nc.vector.tensor_copy(hid16[:, PACK * start + t : PACK * stop : PACK], hid[t][:, start:stop])

        for t in early:
            fetch(pick_b, rows_b, idx4, sb_t, t)

        rows_a = [held("a%d" % t, J, F32) for t in range(2)]
        for h in range(2):
            nc.vector.tensor_copy(rows_a[0][:, halves[h]], product_a(bank(3 + h), 0, halves[h]))
        fetch(pick_a, rows_a, idx3, sa_t, 0)
        nc.vector.tensor_copy(rows_a[1][:], product_a(bank(5), 1, whole))
        fetch(pick_a, rows_a, idx3, sa_t, 1)
        place(0)
        rows_a.append(held("a2", J, F32, after="pick_a0"))
        nc.vector.tensor_copy(rows_a[2][:], product_a(bank(6), 2, whole))
        fetch(pick_a, rows_a, idx3, sa_t, 2)
        cleared_page(1, after="a1")
        place(1)
        rows_b.append(held("b3", J, F32, after="pick_b0"))
        acc_b3 = bank(3)
        for h in range(2):
            product_b(acc_b3, 3, h)
        nc.vector.tensor_copy(rows_b[3][:], acc_b3[:])
        rows_a.append(held("a3", J, F32, after="pick_a1"))
        nc.vector.tensor_copy(rows_a[3][:], product_a(bank(7), 3, whole))
        fetch(pick_b, rows_b, idx4, sb_t, 3)
        fetch(pick_a, rows_a, idx3, sa_t, 3)
        cleared_page(2, after="a0")
        vs_gw = held("vs_gw", N, U16, after="pick_b1")
        vs_gs = held("vs_gs", N, U8, after="larger0")
        gather(vs_gw[:], vs_w, idx6[:])
        gather(vs_gs[:], vs_s, idx6[:])
        round_into_hid16(0)
        place(2)
        cleared_page(3, after="xo_w")
        place(3)
        round_into_hid16(1)
        round_into_hid16(2)

        pieces = C // P

        def finish(piece):
            hq_w = held("hq_w%d" % piece, P, U32)
            hq_s = held("hq_s%d" % piece, P, U8)
            nc.vector.quantize_mx(
                out=hq_w[:].bitcast(FP8X4), scales=hq_s[:], in_=hid16[:, PACK * piece * P : PACK * (piece + 1) * P]
            )
            cols = slice(piece * P, (piece + 1) * P)
            last = piece == pieces - 1
            acc = bank(piece)
            for j in range(N // P):
                if last and j == 1:
                    acc = bank(pieces)
                nc.tensor.matmul_mx(
                    out=acc[:, j * P : (j + 1) * P],
                    lhsT=vs_gw[:, j * P : (j + 1) * P].bitcast(FP4X4),
                    lhsT_scale=vs_gs[:, j * P : (j + 1) * P],
                    rhs=hq_w[:].bitcast(FP8X4),
                    rhs_scale=hq_s[:],
                    start=True,
                    stop=True,
                )
                if last:
                    res = held("res_last%d" % j, P, F32)
                    if j == 0:
                        nc.vector.tensor_copy(res[:], acc[:, 0:P])
                        nc.sync.dma_start(out[0:P, cols], res[:])
                    else:
                        nc.scalar.activation(out=res[:], in_=acc[:, P:N], func=COPY)
                        nc.sync.dma_start(out[P:N, cols], res[:])
            if not last:
                res = held("res%d" % piece, N, F32)
                nc.scalar.activation(out=res[:], in_=acc[:, 0:N], func=COPY)
                nc.sync.dma_start(out[:, cols].rearrange("(j p) c -> p j c", p=P), res[:].rearrange("p (j c) -> p j c", j=2))

        round_into_hid16(PACK - 1, 0, P)
        for piece in range(pieces):
            if piece + 1 < pieces:
                round_into_hid16(PACK - 1, (piece + 1) * P, (piece + 2) * P)
            finish(piece)
